import numpy as np
import ml_dtypes


def mxq(x, axis, fmt="e4m3"):
    dtype, down = {"e4m3": (ml_dtypes.float8_e4m3fn, 7), "e5m2": (ml_dtypes.float8_e5m2, 14)}[fmt]
    v = np.moveaxis(np.asarray(x, np.float32).astype(ml_dtypes.bfloat16).astype(np.float64), axis, -1)
    blocks = v.reshape(v.shape[:-1] + (-1, 32))
    amax = np.abs(blocks).max(-1, keepdims=True)
    byte = np.maximum(np.where(amax > 0, np.frexp(amax)[1] - 1 + 127, 0) - down, 1)
    scale = np.exp2(byte - 127.0)
    codes = (blocks / scale).astype(np.float32).astype(dtype).astype(np.float64)
    return np.moveaxis((codes * scale).reshape(v.shape), -1, axis)


WIDE = False


def mx_kscale(k):
    if not WIDE:
        return np.ones(k)
    levels = np.array([10, -10, 5, -5, 0])
    if k % 512:
        return np.exp2(np.random.permutation(np.resize(levels, k // 32))).repeat(32)
    a = np.empty((k // 512, 16))
    for p in range(k // 512):
        a[p, :8] = np.random.permutation(np.resize(levels, 8))
        for g in range(8):
            far = levels[np.abs(levels - a[p, g]) >= 10]
            a[p, g + 8] = far[np.random.randint(len(far))]
    return np.exp2(a.ravel()).repeat(32)


def f64(x):
    return np.asarray(x).astype(np.float64)


def striped(idx):
    return np.tile(np.asarray(idx).reshape(-1, 16).T, (8, 1)).astype(np.uint16)


def unstriped(offs):
    return offs[:16].T.reshape(-1).astype(np.int64)


E2M1 = np.array([0.0, 0.5, 1.0, 1.5, 2.0, 3.0, 4.0, 6.0, -0.0, -0.5, -1.0, -1.5, -2.0, -3.0, -4.0, -6.0])


def pack_weight(w, fmt):
    k, n = w.shape
    w = f64(np.asarray(w, np.float32).astype(ml_dtypes.bfloat16)).reshape(k // 32, 32, n)
    amax = np.abs(w).max(1)
    if fmt == "e4m3":
        byte = np.frexp(amax)[1] - 1 + 127 - 7
    else:
        mant, ex = np.frexp(amax / 6.0)
        byte = np.where(mant > 0.5, ex, ex - 1) + 127
    byte = np.clip(np.where(amax > 0, byte, 1), 1, 254)
    scaled = (w * np.exp2(127.0 - byte)[:, None, :]).reshape(k, n).astype(np.float32)
    by_word = np.ascontiguousarray(scaled.reshape(k // 512, 128, 4, n).transpose(0, 1, 3, 2))
    if fmt == "e4m3":
        words = by_word.astype(ml_dtypes.float8_e4m3fn).view(np.uint8)
    else:
        c = by_word.astype(ml_dtypes.float4_e2m1fn).view(np.uint8) & 0xF
        words = (c[..., 0::2] | (c[..., 1::2] << 4)).reshape(k // 512, 128, 2 * n)
    return np.ascontiguousarray(words), np.ascontiguousarray(byte.astype(np.uint8).reshape(k // 512, 16, n))


def unpack_weight(words, scales, fmt):
    g, _, n = scales.shape
    words = np.ascontiguousarray(words).reshape(g, 128, n, -1)
    if fmt == "e4m3":
        vals = words.view(ml_dtypes.float8_e4m3fn).astype(np.float64)
    else:
        nib = np.empty((g, 128, n, 4), np.uint8)
        nib[..., 0::2] = words & 0xF
        nib[..., 1::2] = words >> 4
        vals = E2M1[nib]
    vals = vals * np.repeat(np.exp2(scales.astype(np.float64) - 127.0), 8, axis=1)[..., None]
    return vals.transpose(0, 1, 3, 2).reshape(g * 512, n)


def softplus(v):
    return np.log(1.0 + np.exp(v))


def bf(x):
    return np.asarray(x, np.float32).astype(ml_dtypes.bfloat16)


def planes(Y):
    r, m = Y.shape
    b = f64(bf(Y)).reshape(r // 32, 32, m)
    amax = np.abs(b).max(1)
    byte = np.clip(np.where(amax > 0, np.frexp(amax)[1] - 1 + 127 - 7, 1), 1, 254)
    codes = (b * np.exp2(127.0 - byte)[:, None, :]).reshape(r, m).astype(np.float32).astype(ml_dtypes.float8_e4m3fn).view(np.uint8)
    words = codes.reshape(r // 512, 128, 4, m).transpose(0, 1, 3, 2)
    return np.ascontiguousarray(words), np.ascontiguousarray(byte.astype(np.uint8).reshape(r // 512, 16, m))


K, T, J, B, L, N = 1024, 2048, 512, 128, 512, 512


def setup_inputs():
    n = np.random.standard_normal
    idx = np.random.permutation(T)[:J]
    fk = mx_kscale(K)
    fl = mx_kscale(L)
    wap = pack_weight(n((K, N)) * 1 / np.sqrt(K) * fk[:, None], "e2m1")
    cxp = pack_weight(n((L, B)) / fl[:, None], "e4m3")
    wcp = pack_weight(n((L, N)) * 1 / np.sqrt(L) * fl[:, None], "e2m1")
    return {
        "xq": (n((K, T)) / fk[:, None]).astype(np.float32),
        "wa_words": wap[0],
        "wa_scales": wap[1],
        "ga": (np.random.uniform(0.4, 1.2, (1, J))).astype(np.float32),
        "cx_words": cxp[0],
        "cx_scales": cxp[1],
        "wc_words": wcp[0],
        "wc_scales": wcp[1],
        "offs": striped(idx),
    }


def reference(xq, wa_words, wa_scales, ga, cx_words, cx_scales, wc_words, wc_scales, offs):
    idx = unstriped(offs)
    wau = unpack_weight(wa_words, wa_scales, "e2m1")
    cxu = unpack_weight(cx_words, cx_scales, "e4m3")
    wcu = unpack_weight(wc_words, wc_scales, "e2m1")
    xqidxq = mxq(f64(xq)[:, idx], 0, "e4m3")
    p = wau.T @ xqidxq
    w = softplus(p) * f64(ga)
    s = w.reshape(N, B, J // B).sum(axis=2)
    q = wcu.T @ cxu
    y = s + q
    words, scales = planes(y)
    return y, words, scales

@@ -1,0 +1,219 @@
+from contextlib import ExitStack
+
+import concourse.mybir as mybir
+from concourse.masks import make_identity
+
+K, T, J, B, L, N = 1024, 2048, 512, 128, 512, 512
+FLOPS = 2 * K * N * J + 2 * L * N * B
+
+F32 = mybir.dt.float32
+BF16 = mybir.dt.bfloat16
+I32 = mybir.dt.int32
+U32 = mybir.dt.uint32
+U16 = mybir.dt.uint16
+U8 = mybir.dt.uint8
+FP8X4 = mybir.dt.float8_e4m3fn_x4
+FP4X4 = mybir.dt.float4_e2m1fn_x4
+ALU = mybir.AluOpType
+ACT = mybir.ActivationFunctionType
+
+P = 128
+PACK = 4
+K_PASS = P * PACK
+PASSES = K // K_PASS
+GROUP = J // B
+LIST_COLS = J // 16
+CAP = 30.0
+
+
+def load_scale_rows(nc, tile, rows, quadrants):
+    for q in quadrants:
+        nc.sync.dma_start(
+            out=tile[32 * q : 32 * q + 4].bitcast(I32),
+            in_=rows[:, 4 * q : 4 * q + 4, :].rearrange("z q c -> q z c").bitcast(I32),
+        )
+
+
+def tile_list_expert_then_pool_pl_kernel(
+    tc, xq, wa_words, wa_scales, ga, cx_words, cx_scales, wc_words, wc_scales, offs, out_0, out_1, out_2
+):
+    nc = tc.nc
+    with ExitStack() as ctx:
+        sb = ctx.enter_context(tc.tile_pool(name="sb", bufs=1))
+        ps = ctx.enter_context(tc.psum_pool(name="ps", bufs=1))
+
+        offsets = sb.tile([P, LIST_COLS], U16, name="offsets")
+        rows = [
+            [sb.tile([P, T], F32, name=f"rows{a}{t}") for t in range(PACK)] for a in range(PASSES)
+        ]
+        wa = sb.tile([P, PASSES, 2 * N], U8, name="wa", align_bytes=64)
+        wc = sb.tile([P, 2 * N], U8, name="wc", align_bytes=64)
+        cx = sb.tile([P, B], U32, name="cx", align_bytes=64)
+        wa_sc = sb.tile([P, PASSES, N], U8, name="wa_sc", align_bytes=64)
+        wc_sc = sb.tile([P, 1, N], U8, name="wc_sc", align_bytes=64)
+        cx_sc = sb.tile([P, 1, B], U8, name="cx_sc", align_bytes=64)
+        gate = sb.tile([P, GROUP], F32, name="gate")
+        ident = sb.tile([P, P], F32, name="ident")
+
+        def load_rows(a, t):
+            src = xq[a * K_PASS : (a + 1) * K_PASS, :].rearrange("(p t) c -> p t c", t=PACK)
+            nc.sync.dma_start(out=rows[a][t][:], in_=src[:, t, :])
+
+        for plane in (wa_sc, wc_sc, cx_sc):
+            nc.vector.memset(plane[:].bitcast(I32), 0)
+        make_identity(nc, ident[:])
+
+        load_rows(0, 0)
+        nc.sync.dma_start(offsets[:], offs)
+        load_rows(0, 1)
+        nc.sync.dma_start(out=wa[:].bitcast(I32), in_=wa_words.rearrange("z p c -> p z c").bitcast(I32))
+        load_rows(0, 2)
+        load_scale_rows(nc, wa_sc, wa_scales, (0, 1))
+        load_rows(0, 3)
+        load_scale_rows(nc, wa_sc, wa_scales, (2, 3))
+        for t in range(PACK):
+            load_rows(1, t)
+        nc.sync.dma_start(out=gate[:], in_=ga[0].rearrange("(b r) -> b r", r=GROUP))
+        nc.sync.dma_start(out=wc[:].bitcast(I32), in_=wc_words[0].bitcast(I32))
+        nc.sync.dma_start(
+            out=cx[:].bitcast(I32), in_=cx_words[0].rearrange("p c r -> p (c r)").bitcast(I32)
+        )
+        load_scale_rows(nc, wc_sc, wc_scales, range(4))
+        load_scale_rows(nc, cx_sc, cx_scales, range(4))
+
+        p_ps = [ps.tile([P, N], F32, name=f"p_ps{r}", tag=f"p{r}") for r in range(GROUP)]
+        half = J // 2
+        for a in range(PASSES):
+            picked = sb.tile([P, PACK, J], BF16, name=f"picked{a}")
+            woven = [
+                sb.tile([P, B, PACK], BF16, name=f"woven{a}{r}", align_bytes=64) for r in range(GROUP)
+            ]
+            for t in range(PACK):
+                window = rows[a][t][:]
+                nc.vector.tensor_copy(
+                    out=picked[:, t, :half], in_=window.indirect(offsets[:, : LIST_COLS // 2])
+                )
+                nc.scalar.activation(
+                    out=picked[:, t, half:], in_=window.indirect(offsets[:, LIST_COLS // 2 :]), func=ACT.Copy
+                )
+                if t % 2 == 1:
+                    pair = picked[:, t - 1 : t + 1, :].rearrange("p t (b r) -> p r b t", r=GROUP)
+                    for r in range(GROUP):
+                        dst = woven[r][:, :, t - 1 : t + 1]
+                        if r < GROUP // 2:
+                            nc.vector.tensor_copy(out=dst, in_=pair[:, r])
+                        else:
+                            nc.scalar.copy(out=dst, in_=pair[:, r])
+            for r in range(GROUP):
+                codes = sb.tile([P, B], U32, name=f"codes{a}{r}", align_bytes=64)
+                scales = sb.tile([P, B], U8, name=f"scales{a}{r}", align_bytes=64)
+                nc.vector.quantize_mx(
+                    out=codes[:].bitcast(FP8X4),
+                    scales=scales[:],
+                    in_=woven[r][:].rearrange("p b t -> p (b t)"),
+                )
+                nc.tensor.matmul_mx(
+                    out=p_ps[r][:],
+                    lhsT=codes[:].bitcast(FP8X4),
+                    lhsT_scale=scales[:],
+                    rhs=wa[:, a, :].bitcast(FP4X4),
+                    rhs_scale=wa_sc[:, a, :],
+                    start=(a == 0),
+                    stop=(a == PASSES - 1),
+                )
+
+        dealt = [p_ps[r][:].rearrange("p (c t) -> p t c", t=PACK) for r in range(GROUP)]
+        work = sb.tile([P, GROUP * N], F32, name="work")
+        capped = work[:].rearrange("p (r t c) -> p r t c", r=GROUP, t=PACK)
+        logs = work[:].rearrange("p (t r c) -> p r t c", r=GROUP, t=PACK)
+        exps = sb.tile([P, GROUP, PACK, P], F32, name="exps")
+        for r in range(GROUP):
+            nc.vector.tensor_scalar(
+                out=capped[:, r], in0=dealt[r], scalar1=CAP, scalar2=None, op0=ALU.min
+            )
+            nc.scalar.activation(out=exps[:, r], in_=capped[:, r], func=ACT.Exp)
+
+        y_ps = [ps.tile([P, B], F32, name=f"y_ps{t}", tag=f"y{t}") for t in range(PACK)]
+        excess = [sb.tile([P, PACK, P], F32, name=f"excess{r}") for r in range(GROUP)]
+        excess_w = [sb.tile([P, PACK, P], F32, name=f"excess_w{r}") for r in range(GROUP)]
+
+        def weigh_excess(r):
+            nc.vector.tensor_scalar(
+                out=excess_w[r][:], in0=excess[r][:], scalar1=gate[:, r : r + 1], scalar2=None, op0=ALU.mult
+            )
+            for t in range(PACK):
+                nc.tensor.matmul(
+                    y_ps[t][:], excess_w[r][:, t, :], ident[:], start=(r == 0), stop=False, is_transpose=True
+                )
+
+        for r in range(GROUP):
+            nc.vector.tensor_scalar(
+                out=excess[r][:], in0=dealt[r], scalar1=CAP, scalar2=0.0, op0=ALU.subtract, op1=ALU.max
+            )
+            if r > 0:
+                weigh_excess(r - 1)
+        weigh_excess(GROUP - 1)
+
+        q_ps = ps.tile([P, N], F32, name="q_ps", tag="p0")
+        nc.tensor.matmul_mx(
+            out=q_ps[:],
+            lhsT=cx[:].bitcast(FP8X4),
+            lhsT_scale=cx_sc[:, 0, :],
+            rhs=wc[:].bitcast(FP4X4),
+            rhs_scale=wc_sc[:, 0, :],
+            start=True,
+            stop=True,
+        )
+
+        total = q_ps[:].rearrange("p (c t) -> p t c", t=PACK)
+        for r in range(GROUP):
+            last = r == GROUP - 1
+            step = 1 if last else PACK // 2
+            new_total = sb.tile([P, PACK, P], F32, name=f"total{r}")
+            if not last:
+                nc.scalar.activation(out=logs[:, r], in_=exps[:, r], func=ACT.Ln, bias=1.0)
+            for t0 in range(0, PACK, step):
+                ts = slice(t0, t0 + step)
+                if last:
+                    nc.scalar.activation(out=logs[:, r, ts], in_=exps[:, r, ts], func=ACT.Ln, bias=1.0)
+                nc.vector.scalar_tensor_tensor(
+                    out=new_total[:, ts],
+                    in0=logs[:, r, ts],
+                    scalar=gate[:, r : r + 1],
+                    in1=total[:, ts],
+                    op0=ALU.mult,
+                    op1=ALU.add,
+                )
+            total = new_total[:]
+
+        y_sb = sb.tile([P, PACK, B], F32, name="y_sb")
+        y_woven = sb.tile([P, B, PACK], BF16, name="y_woven", align_bytes=64)
+        for t in range(PACK):
+            nc.tensor.matmul(
+                y_ps[t][:], total[:, t, :], ident[:], start=False, stop=True, is_transpose=True
+            )
+        for t in range(PACK):
+            nc.scalar.copy(out=y_sb[:, t, :], in_=y_ps[t][:])
+            if t % 2 == 1:
+                nc.vector.tensor_copy(
+                    out=y_woven[:, :, t - 1 : t + 1],
+                    in_=y_sb[:, t - 1 : t + 1, :].rearrange("p t b -> p b t"),
+                )
+        nc.sync.dma_start(out=out_0.rearrange("(p t) b -> p t b", t=PACK), in_=y_sb[:])
+
+        y_codes = sb.tile([P, B], U32, name="y_codes", align_bytes=64)
+        y_scales = sb.tile([P, B], U8, name="y_scales", align_bytes=64)
+        nc.vector.quantize_mx(
+            out=y_codes[:].bitcast(FP8X4),
+            scales=y_scales[:],
+            in_=y_woven[:].rearrange("p b t -> p (b t)"),
+        )
+        nc.sync.dma_start(
+            out=out_1[0].rearrange("p c r -> p (c r)").bitcast(I32), in_=y_codes[:].bitcast(I32)
+        )
+        for q in range(4):
+            queue = nc.sync if q % 2 == 0 else nc.scalar
+            queue.dma_start(
+                out=out_2[0, 4 * q : 4 * q + 4, :].bitcast(I32),
+                in_=y_scales[32 * q : 32 * q + 4, :].bitcast(I32),
+            )

@@ -66,20 +66,24 @@ def tile_list_expert_then_pool_pl_kernel(
         load_rows(0, 0)
         nc.sync.dma_start(offsets[:], offs)
         load_rows(0, 1)
-        nc.sync.dma_start(out=wa[:].bitcast(I32), in_=wa_words.rearrange("z p c -> p z c").bitcast(I32))
-        load_rows(0, 2)
         load_scale_rows(nc, wa_sc, wa_scales, (0, 1))
-        load_rows(0, 3)
+        load_rows(0, 2)
         load_scale_rows(nc, wa_sc, wa_scales, (2, 3))
-        for t in range(PACK):
-            load_rows(1, t)
+        load_rows(0, 3)
+        load_scale_rows(nc, wc_sc, wc_scales, (0, 1))
+        load_rows(1, 0)
+        load_scale_rows(nc, wc_sc, wc_scales, (2, 3))
+        load_rows(1, 1)
+        load_scale_rows(nc, cx_sc, cx_scales, (0, 1))
+        load_rows(1, 2)
+        load_scale_rows(nc, cx_sc, cx_scales, (2, 3))
+        nc.sync.dma_start(out=wa[:].bitcast(I32), in_=wa_words.rearrange("z p c -> p z c").bitcast(I32))
+        load_rows(1, PACK - 1)
         nc.sync.dma_start(out=gate[:], in_=ga[0].rearrange("(b r) -> b r", r=GROUP))
         nc.sync.dma_start(out=wc[:].bitcast(I32), in_=wc_words[0].bitcast(I32))
         nc.sync.dma_start(
             out=cx[:].bitcast(I32), in_=cx_words[0].rearrange("p c r -> p (c r)").bitcast(I32)
         )
-        load_scale_rows(nc, wc_sc, wc_scales, range(4))
-        load_scale_rows(nc, cx_sc, cx_scales, range(4))
 
         p_ps = [ps.tile([P, N], F32, name=f"p_ps{r}", tag=f"p{r}") for r in range(GROUP)]
         half = J // 2
@@ -123,49 +127,60 @@ def tile_list_expert_then_pool_pl_kernel(
                 )
 
         dealt = [p_ps[r][:].rearrange("p (c t) -> p t c", t=PACK) for r in range(GROUP)]
-        work = sb.tile([P, GROUP * N], F32, name="work")
-        capped = work[:].rearrange("p (r t c) -> p r t c", r=GROUP, t=PACK)
-        logs = work[:].rearrange("p (t r c) -> p r t c", r=GROUP, t=PACK)
+        early = sb.tile([P, 2, PACK, P], F32, name="early")
+        excess = sb.tile([P, GROUP, PACK, P], F32, name="excess")
+        logs = sb.tile([P, GROUP, PACK, P], F32, name="logs")
+        capped = [early[:, 0], early[:, 1], excess[:, :, 0, :], logs[:, :, 0, :]]
         exps = sb.tile([P, GROUP, PACK, P], F32, name="exps")
         for r in range(GROUP):
-            nc.vector.tensor_scalar(
-                out=capped[:, r], in0=dealt[r], scalar1=CAP, scalar2=None, op0=ALU.min
-            )
-            nc.scalar.activation(out=exps[:, r], in_=capped[:, r], func=ACT.Exp)
+            for cs in (slice(0, P // 2), slice(P // 2, P)):
+                nc.vector.tensor_scalar(
+                    out=capped[r][:, :, cs], in0=dealt[r][:, :, cs], scalar1=CAP, scalar2=None, op0=ALU.min
+                )
+                nc.scalar.activation(out=exps[:, r, :, cs], in_=capped[r][:, :, cs], func=ACT.Exp)
 
         y_ps = [ps.tile([P, B], F32, name=f"y_ps{t}", tag=f"y{t}") for t in range(PACK)]
-        excess = [sb.tile([P, PACK, P], F32, name=f"excess{r}") for r in range(GROUP)]
-        excess_w = [sb.tile([P, PACK, P], F32, name=f"excess_w{r}") for r in range(GROUP)]
-
-        def weigh_excess(r):
+        for r in range(GROUP):
             nc.vector.tensor_scalar(
-                out=excess_w[r][:], in0=excess[r][:], scalar1=gate[:, r : r + 1], scalar2=None, op0=ALU.mult
+                out=excess[:, r], in0=dealt[r], scalar1=CAP, scalar2=0.0, op0=ALU.subtract, op1=ALU.max
+            )
+            if r == 0:
+                q_ps = ps.tile([P, N], F32, name="q_ps", tag="p0")
+                nc.tensor.matmul_mx(
+                    out=q_ps[:],
+                    lhsT=cx[:].bitcast(FP8X4),
+                    lhsT_scale=cx_sc[:, 0, :],
+                    rhs=wc[:].bitcast(FP4X4),
+                    rhs_scale=wc_sc[:, 0, :],
+                    start=True,
+                    stop=True,
+                )
+            if r == GROUP - 1:
+                continue
+            excess_w = sb.tile([P, PACK, P], F32, name=f"excess_w{r}")
+            nc.gpsimd.tensor_scalar(
+                out=excess_w[:],
+                in0=excess[:, r],
+                scalar1=gate[:, r : r + 1],
+                scalar2=0.0,
+                op0=ALU.mult,
+                op1=ALU.add,
             )
             for t in range(PACK):
                 nc.tensor.matmul(
-                    y_ps[t][:], excess_w[r][:, t, :], ident[:], start=(r == 0), stop=False, is_transpose=True
+                    y_ps[t][:], excess_w[:, t, :], ident[:], start=(r == 0), stop=False, is_transpose=True
                 )
 
-        for r in range(GROUP):
-            nc.vector.tensor_scalar(
-                out=excess[r][:], in0=dealt[r], scalar1=CAP, scalar2=0.0, op0=ALU.subtract, op1=ALU.max
-            )
-            if r > 0:
-                weigh_excess(r - 1)
-        weigh_excess(GROUP - 1)
-
-        q_ps = ps.tile([P, N], F32, name="q_ps", tag="p0")
-        nc.tensor.matmul_mx(
-            out=q_ps[:],
-            lhsT=cx[:].bitcast(FP8X4),
-            lhsT_scale=cx_sc[:, 0, :],
-            rhs=wc[:].bitcast(FP4X4),
-            rhs_scale=wc_sc[:, 0, :],
-            start=True,
-            stop=True,
+        seed = sb.tile([P, PACK, P], F32, name="seed")
+        nc.vector.scalar_tensor_tensor(
+            out=seed[:],
+            in0=excess[:, GROUP - 1],
+            scalar=gate[:, GROUP - 1 : GROUP],
+            in1=q_ps[:].rearrange("p (c t) -> p t c", t=PACK),
+            op0=ALU.mult,
+            op1=ALU.add,
         )
-
-        total = q_ps[:].rearrange("p (c t) -> p t c", t=PACK)
+        total = seed[:]
         for r in range(GROUP):
             last = r == GROUP - 1
             step = 1 if last else PACK // 2

@@ -26,11 +26,11 @@ LIST_COLS = J // 16
 CAP = 30.0
 
 
-def load_scale_rows(nc, tile, rows, quadrants):
-    for q in quadrants:
+def load_scale_rows(nc, tile, rows, lanes):
+    for i in lanes:
         nc.sync.dma_start(
-            out=tile[32 * q : 32 * q + 4].bitcast(I32),
-            in_=rows[:, 4 * q : 4 * q + 4, :].rearrange("z q c -> q z c").bitcast(I32),
+            out=tile[i:P:32].bitcast(I32),
+            in_=rows[:, i:16:4, :].rearrange("z q c -> q z c").bitcast(I32),
         )
 
 
@@ -65,6 +65,7 @@ def tile_list_expert_then_pool_pl_kernel(
 
         load_rows(0, 0)
         nc.sync.dma_start(offsets[:], offs)
+        nc.sync.dma_start(out=gate[:], in_=ga[0].rearrange("(b r) -> b r", r=GROUP))
         load_rows(0, 1)
         load_scale_rows(nc, wa_sc, wa_scales, (0, 1))
         load_rows(0, 2)
@@ -79,7 +80,6 @@ def tile_list_expert_then_pool_pl_kernel(
         load_scale_rows(nc, cx_sc, cx_scales, (2, 3))
         nc.sync.dma_start(out=wa[:].bitcast(I32), in_=wa_words.rearrange("z p c -> p z c").bitcast(I32))
         load_rows(1, PACK - 1)
-        nc.sync.dma_start(out=gate[:], in_=ga[0].rearrange("(b r) -> b r", r=GROUP))
         nc.sync.dma_start(out=wc[:].bitcast(I32), in_=wc_words[0].bitcast(I32))
         nc.sync.dma_start(
             out=cx[:].bitcast(I32), in_=cx_words[0].rearrange("p c r -> p (c r)").bitcast(I32)
@@ -130,67 +130,62 @@ def tile_list_expert_then_pool_pl_kernel(
         early = sb.tile([P, 2, PACK, P], F32, name="early")
         excess = sb.tile([P, GROUP, PACK, P], F32, name="excess")
         logs = sb.tile([P, GROUP, PACK, P], F32, name="logs")
-        capped = [early[:, 0], early[:, 1], excess[:, :, 0, :], logs[:, :, 0, :]]
+        capped = [early[:, 0], excess[:, :, 0, :], early[:, 1], logs[:, :, 0, :]]
         exps = sb.tile([P, GROUP, PACK, P], F32, name="exps")
-        for r in range(GROUP):
-            for cs in (slice(0, P // 2), slice(P // 2, P)):
-                nc.vector.tensor_scalar(
-                    out=capped[r][:, :, cs], in0=dealt[r][:, :, cs], scalar1=CAP, scalar2=None, op0=ALU.min
-                )
-                nc.scalar.activation(out=exps[:, r, :, cs], in_=capped[r][:, :, cs], func=ACT.Exp)
+        halves = (slice(0, PACK // 2), slice(PACK // 2, PACK))
+        for ts in halves:
+            nc.scalar.activation(out=capped[0][:, ts], in_=dealt[0][:, ts], func=ACT.Abs)
+        for ts in halves:
+            nc.scalar.activation(out=exps[:, 0, ts], in_=capped[0][:, ts], func=ACT.Exp, scale=-1.0)
+        for r in range(1, GROUP):
+            nc.vector.tensor_scalar(
+                out=capped[r], in0=dealt[r], scalar1=CAP, scalar2=None, op0=ALU.min
+            )
+            nc.scalar.activation(out=exps[:, r], in_=capped[r], func=ACT.Exp)
+
+        nc.vector.tensor_scalar(
+            out=excess[:, 0], in0=dealt[0], scalar1=0.0, scalar2=gate[:, 0:1], op0=ALU.max, op1=ALU.mult
+        )
+        q_ps = ps.tile([P, N], F32, name="q_ps", tag="p0")
+        nc.tensor.matmul_mx(
+            out=q_ps[:],
+            lhsT=cx[:].bitcast(FP8X4),
+            lhsT_scale=cx_sc[:, 0, :],
+            rhs=wc[:].bitcast(FP4X4),
+            rhs_scale=wc_sc[:, 0, :],
+            start=True,
+            stop=True,
+        )
 
         y_ps = [ps.tile([P, B], F32, name=f"y_ps{t}", tag=f"y{t}") for t in range(PACK)]
         for r in range(GROUP):
-            nc.vector.tensor_scalar(
-                out=excess[:, r], in0=dealt[r], scalar1=CAP, scalar2=0.0, op0=ALU.subtract, op1=ALU.max
-            )
-            if r == 0:
-                q_ps = ps.tile([P, N], F32, name="q_ps", tag="p0")
-                nc.tensor.matmul_mx(
-                    out=q_ps[:],
-                    lhsT=cx[:].bitcast(FP8X4),
-                    lhsT_scale=cx_sc[:, 0, :],
-                    rhs=wc[:].bitcast(FP4X4),
-                    rhs_scale=wc_sc[:, 0, :],
-                    start=True,
-                    stop=True,
+            term = excess[:, r]
+            if r > 0:
+                nc.vector.tensor_scalar(
+                    out=excess[:, r], in0=dealt[r], scalar1=CAP, scalar2=0.0, op0=ALU.subtract, op1=ALU.max
                 )
-            if r == GROUP - 1:
-                continue
-            excess_w = sb.tile([P, PACK, P], F32, name=f"excess_w{r}")
-            nc.gpsimd.tensor_scalar(
-                out=excess_w[:],
-                in0=excess[:, r],
-                scalar1=gate[:, r : r + 1],
-                scalar2=0.0,
-                op0=ALU.mult,
-                op1=ALU.add,
-            )
+                weighted = sb.tile([P, PACK, P], F32, name=f"weighted{r}")
+                nc.gpsimd.tensor_scalar(
+                    out=weighted[:],
+                    in0=excess[:, r],
+                    scalar1=gate[:, r : r + 1],
+                    scalar2=0.0,
+                    op0=ALU.mult,
+                    op1=ALU.add,
+                )
+                term = weighted[:]
             for t in range(PACK):
                 nc.tensor.matmul(
-                    y_ps[t][:], excess_w[:, t, :], ident[:], start=(r == 0), stop=False, is_transpose=True
+                    y_ps[t][:], term[:, t, :], ident[:], start=(r == 0), stop=False, is_transpose=True
                 )
 
-        seed = sb.tile([P, PACK, P], F32, name="seed")
-        nc.vector.scalar_tensor_tensor(
-            out=seed[:],
-            in0=excess[:, GROUP - 1],
-            scalar=gate[:, GROUP - 1 : GROUP],
-            in1=q_ps[:].rearrange("p (c t) -> p t c", t=PACK),
-            op0=ALU.mult,
-            op1=ALU.add,
-        )
-        total = seed[:]
+        total = q_ps[:].rearrange("p (c t) -> p t c", t=PACK)
         for r in range(GROUP):
-            last = r == GROUP - 1
-            step = 1 if last else PACK // 2
+            step = 1 if r == GROUP - 1 else PACK // 2
             new_total = sb.tile([P, PACK, P], F32, name=f"total{r}")
-            if not last:
-                nc.scalar.activation(out=logs[:, r], in_=exps[:, r], func=ACT.Ln, bias=1.0)
             for t0 in range(0, PACK, step):
                 ts = slice(t0, t0 + step)
-                if last:
-                    nc.scalar.activation(out=logs[:, r, ts], in_=exps[:, r, ts], func=ACT.Ln, bias=1.0)
+                nc.scalar.activation(out=logs[:, r, ts], in_=exps[:, r, ts], func=ACT.Ln, bias=1.0)
                 nc.vector.scalar_tensor_tensor(
                     out=new_total[:, ts],
                     in0=logs[:, r, ts],

from contextlib import ExitStack

import concourse.mybir as mybir
from concourse.masks import make_identity

K, T, J, B, L, N = 1024, 2048, 512, 128, 512, 512
FLOPS = 2 * K * N * J + 2 * L * N * B

F32 = mybir.dt.float32
BF16 = mybir.dt.bfloat16
I32 = mybir.dt.int32
U32 = mybir.dt.uint32
U16 = mybir.dt.uint16
U8 = mybir.dt.uint8
FP8X4 = mybir.dt.float8_e4m3fn_x4
FP4X4 = mybir.dt.float4_e2m1fn_x4
ALU = mybir.AluOpType
ACT = mybir.ActivationFunctionType

P = 128
PACK = 4
K_PASS = P * PACK
PASSES = K // K_PASS
GROUP = J // B
LIST_COLS = J // 16
CAP = 30.0


def load_scale_rows(nc, tile, rows, lanes):
    for i in lanes:
        nc.sync.dma_start(
            out=tile[i:P:32].bitcast(I32),
            in_=rows[:, i:16:4, :].rearrange("z q c -> q z c").bitcast(I32),
        )


def tile_list_expert_then_pool_pl_kernel(
    tc, xq, wa_words, wa_scales, ga, cx_words, cx_scales, wc_words, wc_scales, offs, out_0, out_1, out_2
):
    nc = tc.nc
    with ExitStack() as ctx:
        sb = ctx.enter_context(tc.tile_pool(name="sb", bufs=1))
        ps = ctx.enter_context(tc.psum_pool(name="ps", bufs=1))

        offsets = sb.tile([P, LIST_COLS], U16, name="offsets")
        rows = [
            [sb.tile([P, T], F32, name=f"rows{a}{t}") for t in range(PACK)] for a in range(PASSES)
        ]
        wa = sb.tile([P, PASSES, 2 * N], U8, name="wa", align_bytes=64)
        wc = sb.tile([P, 2 * N], U8, name="wc", align_bytes=64)
        cx = sb.tile([P, B], U32, name="cx", align_bytes=64)
        wa_sc = sb.tile([P, PASSES, N], U8, name="wa_sc", align_bytes=64)
        wc_sc = sb.tile([P, 1, N], U8, name="wc_sc", align_bytes=64)
        cx_sc = sb.tile([P, 1, B], U8, name="cx_sc", align_bytes=64)
        gate = sb.tile([P, GROUP], F32, name="gate")
        ident = sb.tile([P, P], F32, name="ident")

        def load_rows(a, t):
            src = xq[a * K_PASS : (a + 1) * K_PASS, :].rearrange("(p t) c -> p t c", t=PACK)
            nc.sync.dma_start(out=rows[a][t][:], in_=src[:, t, :])

        for plane in (wa_sc, wc_sc, cx_sc):
            nc.vector.memset(plane[:].bitcast(I32), 0)
        make_identity(nc, ident[:])

        load_rows(0, 0)
        nc.sync.dma_start(offsets[:], offs)
        nc.sync.dma_start(out=gate[:], in_=ga[0].rearrange("(b r) -> b r", r=GROUP))
        load_rows(0, 1)
        load_scale_rows(nc, wa_sc, wa_scales, (0, 1))
        load_rows(0, 2)
        load_scale_rows(nc, wa_sc, wa_scales, (2, 3))
        load_rows(0, 3)
        load_scale_rows(nc, wc_sc, wc_scales, (0, 1))
        load_rows(1, 0)
        load_scale_rows(nc, wc_sc, wc_scales, (2, 3))
        load_rows(1, 1)
        load_scale_rows(nc, cx_sc, cx_scales, (0, 1))
        load_rows(1, 2)
        load_scale_rows(nc, cx_sc, cx_scales, (2, 3))
        nc.sync.dma_start(out=wa[:].bitcast(I32), in_=wa_words.rearrange("z p c -> p z c").bitcast(I32))
        load_rows(1, PACK - 1)
        nc.sync.dma_start(out=wc[:].bitcast(I32), in_=wc_words[0].bitcast(I32))
        nc.sync.dma_start(
            out=cx[:].bitcast(I32), in_=cx_words[0].rearrange("p c r -> p (c r)").bitcast(I32)
        )

        p_ps = [ps.tile([P, N], F32, name=f"p_ps{r}", tag=f"p{r}") for r in range(GROUP)]
        half = J // 2
        for a in range(PASSES):
            picked = sb.tile([P, PACK, J], BF16, name=f"picked{a}")
            woven = [
                sb.tile([P, B, PACK], BF16, name=f"woven{a}{r}", align_bytes=64) for r in range(GROUP)
            ]
            for t in range(PACK):
                window = rows[a][t][:]
                nc.vector.tensor_copy(
                    out=picked[:, t, :half], in_=window.indirect(offsets[:, : LIST_COLS // 2])
                )
                nc.scalar.activation(
                    out=picked[:, t, half:], in_=window.indirect(offsets[:, LIST_COLS // 2 :]), func=ACT.Copy
                )
                if t % 2 == 1:
                    pair = picked[:, t - 1 : t + 1, :].rearrange("p t (b r) -> p r b t", r=GROUP)
                    for r in range(GROUP):
                        dst = woven[r][:, :, t - 1 : t + 1]
                        if r < GROUP // 2:
                            nc.vector.tensor_copy(out=dst, in_=pair[:, r])
                        else:
                            nc.scalar.copy(out=dst, in_=pair[:, r])
            for r in range(GROUP):
                codes = sb.tile([P, B], U32, name=f"codes{a}{r}", align_bytes=64)
                scales = sb.tile([P, B], U8, name=f"scales{a}{r}", align_bytes=64)
                nc.vector.quantize_mx(
                    out=codes[:].bitcast(FP8X4),
                    scales=scales[:],
                    in_=woven[r][:].rearrange("p b t -> p (b t)"),
                )
                nc.tensor.matmul_mx(
                    out=p_ps[r][:],
                    lhsT=codes[:].bitcast(FP8X4),
                    lhsT_scale=scales[:],
                    rhs=wa[:, a, :].bitcast(FP4X4),
                    rhs_scale=wa_sc[:, a, :],
                    start=(a == 0),
                    stop=(a == PASSES - 1),
                )

        dealt = [p_ps[r][:].rearrange("p (c t) -> p t c", t=PACK) for r in range(GROUP)]
        early = sb.tile([P, 2, PACK, P], F32, name="early")
        excess = sb.tile([P, GROUP, PACK, P], F32, name="excess")
        logs = sb.tile([P, GROUP, PACK, P], F32, name="logs")
        capped = [early[:, 0], excess[:, :, 0, :], early[:, 1], logs[:, :, 0, :]]
        exps = sb.tile([P, GROUP, PACK, P], F32, name="exps")
        halves = (slice(0, PACK // 2), slice(PACK // 2, PACK))
        for ts in halves:
            nc.scalar.activation(out=capped[0][:, ts], in_=dealt[0][:, ts], func=ACT.Abs)
        for ts in halves:
            nc.scalar.activation(out=exps[:, 0, ts], in_=capped[0][:, ts], func=ACT.Exp, scale=-1.0)
        for r in range(1, GROUP):
            nc.vector.tensor_scalar(
                out=capped[r], in0=dealt[r], scalar1=CAP, scalar2=None, op0=ALU.min
            )
            nc.scalar.activation(out=exps[:, r], in_=capped[r], func=ACT.Exp)

        nc.vector.tensor_scalar(
            out=excess[:, 0], in0=dealt[0], scalar1=0.0, scalar2=gate[:, 0:1], op0=ALU.max, op1=ALU.mult
        )
        q_ps = ps.tile([P, N], F32, name="q_ps", tag="p0")
        nc.tensor.matmul_mx(
            out=q_ps[:],
            lhsT=cx[:].bitcast(FP8X4),
            lhsT_scale=cx_sc[:, 0, :],
            rhs=wc[:].bitcast(FP4X4),
            rhs_scale=wc_sc[:, 0, :],
            start=True,
            stop=True,
        )

        y_ps = [ps.tile([P, B], F32, name=f"y_ps{t}", tag=f"y{t}") for t in range(PACK)]
        for r in range(GROUP):
            term = excess[:, r]
            if r > 0:
                nc.vector.tensor_scalar(
                    out=excess[:, r], in0=dealt[r], scalar1=CAP, scalar2=0.0, op0=ALU.subtract, op1=ALU.max
                )
                weighted = sb.tile([P, PACK, P], F32, name=f"weighted{r}")
                nc.gpsimd.tensor_scalar(
                    out=weighted[:],
                    in0=excess[:, r],
                    scalar1=gate[:, r : r + 1],
                    scalar2=0.0,
                    op0=ALU.mult,
                    op1=ALU.add,
                )
                term = weighted[:]
            for t in range(PACK):
                nc.tensor.matmul(
                    y_ps[t][:], term[:, t, :], ident[:], start=(r == 0), stop=False, is_transpose=True
                )

        total = q_ps[:].rearrange("p (c t) -> p t c", t=PACK)
        for r in range(GROUP):
            step = 1 if r == GROUP - 1 else PACK // 2
            new_total = sb.tile([P, PACK, P], F32, name=f"total{r}")
            for t0 in range(0, PACK, step):
                ts = slice(t0, t0 + step)
                nc.scalar.activation(out=logs[:, r, ts], in_=exps[:, r, ts], func=ACT.Ln, bias=1.0)
                nc.vector.scalar_tensor_tensor(
                    out=new_total[:, ts],
                    in0=logs[:, r, ts],
                    scalar=gate[:, r : r + 1],
                    in1=total[:, ts],
                    op0=ALU.mult,
                    op1=ALU.add,
                )
            total = new_total[:]

        y_sb = sb.tile([P, PACK, B], F32, name="y_sb")
        y_woven = sb.tile([P, B, PACK], BF16, name="y_woven", align_bytes=64)
        for t in range(PACK):
            nc.tensor.matmul(
                y_ps[t][:], total[:, t, :], ident[:], start=False, stop=True, is_transpose=True
            )
        for t in range(PACK):
            nc.scalar.copy(out=y_sb[:, t, :], in_=y_ps[t][:])
            if t % 2 == 1:
                nc.vector.tensor_copy(
                    out=y_woven[:, :, t - 1 : t + 1],
                    in_=y_sb[:, t - 1 : t + 1, :].rearrange("p t b -> p b t"),
                )
        nc.sync.dma_start(out=out_0.rearrange("(p t) b -> p t b", t=PACK), in_=y_sb[:])

        y_codes = sb.tile([P, B], U32, name="y_codes", align_bytes=64)
        y_scales = sb.tile([P, B], U8, name="y_scales", align_bytes=64)
        nc.vector.quantize_mx(
            out=y_codes[:].bitcast(FP8X4),
            scales=y_scales[:],
            in_=y_woven[:].rearrange("p b t -> p (b t)"),
        )
        nc.sync.dma_start(
            out=out_1[0].rearrange("p c r -> p (c r)").bitcast(I32), in_=y_codes[:].bitcast(I32)
        )
        for q in range(4):
            queue = nc.sync if q % 2 == 0 else nc.scalar
            queue.dma_start(
                out=out_2[0, 4 * q : 4 * q + 4, :].bitcast(I32),
                in_=y_scales[32 * q : 32 * q + 4, :].bitcast(I32),
            )
